import numpy as np
CORES = [0,1,2,3,4,5,6,7]
N = 8
ROOT = 2
WIDTHS = [64,16,0,96,8,48,32,24]
OFF = [0,64,80,80,176,184,232,264]
C = 288
def setup_inputs(rng):
    return {"x": rng.standard_normal((N, 128, C), dtype=np.float32)}
def reference(x):
    YW = max(WIDTHS)
    y = np.full((N, 128, YW), np.nan, x.dtype)
    for r in range(N):
        y[r][:, :WIDTHS[r]] = x[ROOT][:, OFF[r]:OFF[r] + WIDTHS[r]]
    return {"y": y}

SCRATCH = {
    "stage": ("sbuf", [128, 288], "float32"),
    "land": ("sbuf", [128, 96], "float32"),
}
SEMAPHORES = ["loaded", "read", "arrived", "stored"]

ENGINES = 16


def rank_program(g, core, T, topo):
    rank = T.rank_of(core)
    if rank is None:
        return
    widths = T.tables["WIDTHS"]
    off = T.tables["OFF"]
    total = T.tables["C"]
    root = T.root
    w = widths[rank]

    if rank == root:
        g.sync.dma_start(T.stage[:, 0:total], T.x[:, 0:total]).then_inc(T.sem.loaded, 16)
        g.wait_ge(T.sem.loaded, 16)
        todo = sorted((r for r in range(len(T.cores)) if r != root and widths[r] > 0), key=lambda r: -widths[r])
        for r in todo:
            dst = T.cores[r]
            rid, pid, _se = topo.addr(dst)
            g.remote_dma(
                T.land[:, 0:widths[r]],
                T.stage[:, off[r]:off[r] + widths[r]],
                T.sem.arrived,
                T.sem.read,
                pid,
                rid,
                topo.mask(core, dst),
            )
        if w > 0:
            g.sync.wait_ge(T.sem.loaded, 16)
            g.sync.dma_start(T.y[:, 0:w], T.stage[:, off[rank]:off[rank] + w]).then_inc(T.sem.stored, 16)
            g.sync.wait_ge(T.sem.stored, 16)
        if todo:
            g.wait_ge(T.sem.read, ENGINES * len(todo))
        return

    if w == 0:
        return
    g.sync.wait_ge(T.sem.arrived, ENGINES)
    g.sync.dma_start(T.y[:, 0:w], T.land[:, 0:w]).then_inc(T.sem.stored, 16)
    g.sync.wait_ge(T.sem.stored, 16)
